import numpy as np
import ml_dtypes


def mxq(x, axis, fmt="e4m3"):
    dtype, down = {"e4m3": (ml_dtypes.float8_e4m3fn, 7), "e5m2": (ml_dtypes.float8_e5m2, 14)}[fmt]
    v = np.moveaxis(np.asarray(x, np.float32).astype(ml_dtypes.bfloat16).astype(np.float64), axis, -1)
    blocks = v.reshape(v.shape[:-1] + (-1, 32))
    amax = np.abs(blocks).max(-1, keepdims=True)
    byte = np.maximum(np.where(amax > 0, np.frexp(amax)[1] - 1 + 127, 0) - down, 1)
    scale = np.exp2(byte - 127.0)
    codes = (blocks / scale).astype(np.float32).astype(dtype).astype(np.float64)
    return np.moveaxis((codes * scale).reshape(v.shape), -1, axis)


WIDE = False


def mx_kscale(k):
    if not WIDE:
        return np.ones(k)
    levels = np.array([10, -10, 5, -5, 0])
    if k % 512:
        return np.exp2(np.random.permutation(np.resize(levels, k // 32))).repeat(32)
    a = np.empty((k // 512, 16))
    for p in range(k // 512):
        a[p, :8] = np.random.permutation(np.resize(levels, 8))
        for g in range(8):
            far = levels[np.abs(levels - a[p, g]) >= 10]
            a[p, g + 8] = far[np.random.randint(len(far))]
    return np.exp2(a.ravel()).repeat(32)


def f64(x):
    return np.asarray(x).astype(np.float64)


def striped(idx):
    return np.tile(idx.reshape(-1, 16).T, (8, 1)).astype(np.uint16)


def unstriped(offs):
    return offs[:16].T.reshape(-1).astype(np.int64)


E2M1 = np.array([0.0, 0.5, 1.0, 1.5, 2.0, 3.0, 4.0, 6.0, -0.0, -0.5, -1.0, -1.5, -2.0, -3.0, -4.0, -6.0])


def pack_weight(w, fmt):
    k, n = w.shape
    w = f64(np.asarray(w, np.float32).astype(ml_dtypes.bfloat16)).reshape(k // 32, 32, n)
    amax = np.abs(w).max(1)
    if fmt == "e4m3":
        byte = np.frexp(amax)[1] - 1 + 127 - 7
    else:
        mant, ex = np.frexp(amax / 6.0)
        byte = np.where(mant > 0.5, ex, ex - 1) + 127
    byte = np.clip(np.where(amax > 0, byte, 1), 1, 254)
    scaled = (w * np.exp2(127.0 - byte)[:, None, :]).reshape(k, n).astype(np.float32)
    by_word = np.ascontiguousarray(scaled.reshape(k // 512, 128, 4, n).transpose(0, 1, 3, 2))
    if fmt == "e4m3":
        words = by_word.astype(ml_dtypes.float8_e4m3fn).view(np.uint8)
    else:
        c = by_word.astype(ml_dtypes.float4_e2m1fn).view(np.uint8) & 0xF
        words = (c[..., 0::2] | (c[..., 1::2] << 4)).reshape(k // 512, 128, 2 * n)
    return np.ascontiguousarray(words), np.ascontiguousarray(byte.astype(np.uint8).reshape(k // 512, 16, n))


def unpack_weight(words, scales, fmt):
    g, _, n = scales.shape
    words = np.ascontiguousarray(words).reshape(g, 128, n, -1)
    if fmt == "e4m3":
        vals = words.view(ml_dtypes.float8_e4m3fn).astype(np.float64)
    else:
        nib = np.empty((g, 128, n, 4), np.uint8)
        nib[..., 0::2] = words & 0xF
        nib[..., 1::2] = words >> 4
        vals = E2M1[nib]
    vals = vals * np.repeat(np.exp2(scales.astype(np.float64) - 127.0), 8, axis=1)[..., None]
    return vals.transpose(0, 1, 3, 2).reshape(g * 512, n)


def gelu(v):
    return 0.5 * v * (1.0 + np.tanh(np.sqrt(2.0 / np.pi) * (v + 0.044715 * v**3)))


K, H, N, T, S = 1024, 1024, 256, 4096, 1024

def setup_inputs():
    n = np.random.standard_normal
    s = mx_kscale(K)[:, None]
    u = mx_kscale(H)[:, None]
    tab_words, tab_scales = pack_weight(n((K, T)) * s, "e2m1")
    offs = striped(np.random.permutation(T)[:S])
    offs2 = striped(np.random.permutation(T)[:S])
    w1 = (n((K, H)) / np.sqrt(K) / s).astype(np.float32)
    fade = np.random.uniform(0.3, 0.9, H).astype(np.float32)
    gain = (np.exp(0.3 * n(H)) * u[:, 0]).astype(np.float32)
    w2_words, w2_scales = pack_weight(n((H, N)) / np.sqrt(H) / u, "e2m1")
    return {"tab_words": tab_words, "tab_scales": tab_scales,
            "offs": offs, "offs2": offs2,
            "w1": w1, "fade": fade, "gain": gain,
            "w2_words": w2_words, "w2_scales": w2_scales}

def reference(tab_words, tab_scales, offs, offs2, w1, fade, gain, w2_words, w2_scales):
    TW = unpack_weight(tab_words, tab_scales, "e2m1")
    v = TW[:, unstriped(offs)]
    v2 = TW[:, unstriped(offs2)]
    wq = mxq(f64(w1), 0, "e4m3")
    x1 = wq.T @ v
    x2 = wq.T @ v2
    d = np.abs(x1 - x2)
    like = np.exp(-(f64(fade)[:, None] * d))
    h = f64(gain)[:, None] * like
    hq = mxq(h, 0, "e4m3")
    w2 = unpack_weight(w2_words, w2_scales, "e2m1")
    out = w2.T @ hq
    return out

@@ -1,0 +1,271 @@
+from contextlib import ExitStack
+
+import concourse.mybir as mybir
+
+K, H, N, T, S = 1024, 1024, 256, 4096, 1024
+FLOPS = 2 * K * H * S * 2 + 2 * H * N * S
+
+F32 = mybir.dt.float32
+BF16 = mybir.dt.bfloat16
+I32 = mybir.dt.int32
+U32 = mybir.dt.uint32
+U16 = mybir.dt.uint16
+U8 = mybir.dt.uint8
+FP8X4 = mybir.dt.float8_e4m3fn_x4
+FP4X4 = mybir.dt.float4_e2m1fn_x4
+ALU = mybir.AluOpType
+ACT = mybir.ActivationFunctionType
+
+P = 128
+PACK = 4
+PASS = P * PACK
+HALF = 512
+LN_RANGE = 2.0**64
+
+
+def tile_list_friendship_homophily_kernel(
+    tc, tab_words, tab_scales, offs, offs2, w1, fade, gain, w2_words, w2_scales, out
+):
+    nc = tc.nc
+    with ExitStack() as ctx:
+        keep = ctx.enter_context(tc.tile_pool(name="keep", bufs=1))
+        work = ctx.enter_context(tc.tile_pool(name="work", bufs=2))
+        psum = ctx.enter_context(tc.psum_pool(name="psum", bufs=1))
+
+        lists = []
+        for name, src in (("pupils", offs), ("friends", offs2)):
+            tile = keep.tile([P, S // 16], U16, name=name)
+            nc.sync.dma_start(tile[:], src)
+            lists.append(tile)
+
+        fade_t = keep.tile([P, 2, PACK], F32, name="fade_t")
+        gain_t = keep.tile([P, 2, PACK], F32, name="gain_t")
+        nc.sync.dma_start(out=gain_t[:], in_=gain.rearrange("(b p t) -> p b t", b=2, t=PACK))
+
+        tab_sc = keep.tile([P, T], U8, name="tab_sc", tag="tab_sc", align_bytes=64)
+        for q in range(4):
+            nc.vector.memset(tab_sc[32 * q : 32 * q + 24, :].bitcast(I32), 0)
+            nc.sync.dma_start(
+                out=tab_sc[32 * q + 24 : 32 * q + 32, :].bitcast(I32),
+                in_=tab_scales[:, 4 * q : 4 * q + 4, :].bitcast(I32),
+            )
+
+
+        raw = {}
+
+        def load_w1(a, b, slot):
+            raw[a, b] = keep.tile([P, PACK, PASS], F32, name=f"raw{a}{b}", tag=slot, align_bytes=64)
+            rows = w1[a * PASS : (a + 1) * PASS, b * PASS : (b + 1) * PASS]
+            nc.sync.dma_start(out=raw[a, b][:], in_=rows.rearrange("(p j) c -> p j c", j=PACK))
+
+        load_w1(0, 0, "raw0")
+        nc.sync.dma_start(out=fade_t[:], in_=fade.rearrange("(b p t) -> p b t", b=2, t=PACK))
+        load_w1(1, 0, "raw1")
+        tab_w = []
+        for a in range(2):
+            tile = keep.tile([P, T], U16, name=f"tab_w{a}", align_bytes=64)
+            nc.sync.dma_start(out=tile[:].bitcast(I32), in_=tab_words[a].bitcast(I32))
+            tab_w.append(tile)
+
+        planes = keep.tile([P, 4 * S], U8, name="planes", align_bytes=64)
+        nc.gpsimd.memset(planes[96:128, :].bitcast(I32), 0)
+
+        gain_flat = gain_t[:].rearrange("p b t -> p (b t)")
+        parts = keep.tile([P, 3, 8], F32, name="parts")
+        nc.vector.tensor_scalar(parts[:, 0, :], gain_flat, 1.0 / LN_RANGE, LN_RANGE, ALU.max, ALU.min)
+        nc.vector.tensor_scalar(parts[:, 1, :], gain_flat, LN_RANGE, 1.0 / LN_RANGE, ALU.max, ALU.mult)
+        nc.vector.tensor_scalar(parts[:, 2, :], gain_flat, 1.0 / LN_RANGE, LN_RANGE, ALU.min, ALU.mult)
+        ln_parts = keep.tile([P, 3, 8], F32, name="ln_parts")
+        nc.scalar.activation(ln_parts[:], parts[:], ACT.Ln)
+        warm = keep.tile([P, 1], F32, name="warm")
+        nc.scalar.activation(warm[:], ln_parts[:, 1, 0:1], ACT.Exp)
+        ln_two = keep.tile([P, 8], F32, name="ln_two")
+        ln_gain = keep.tile([P, 8], F32, name="ln_gain")
+        nc.gpsimd.tensor_tensor(ln_two[:], ln_parts[:, 1, :], ln_parts[:, 2, :], ALU.add)
+        nc.gpsimd.tensor_tensor(ln_gain[:], ln_two[:], ln_parts[:, 0, :], ALU.add)
+        neg_fade = keep.tile([P, 8], F32, name="neg_fade")
+        nc.gpsimd.tensor_scalar(neg_fade[:], fade_t[:].rearrange("p b t -> p (b t)"), -1.0, 0.0, ALU.mult, ALU.add)
+
+        sc_got = keep.tile([P, 2 * S], U8, name="sc_got", tag="sc_got", align_bytes=64)
+        for l in range(2):
+            nc.vector.tensor_copy(sc_got[:, l * S : (l + 1) * S], tab_sc[:].indirect(lists[l][:]))
+
+        w_bf = {}
+
+        def weave_w1(a, b, l):
+            w_bf[a, b, l] = keep.tile([P, PACK * PASS], BF16, name=f"w_bf{a}{b}{l}", tag=f"w_bf{a}{b}{l}", align_bytes=64)
+            dst = w_bf[a, b, l][:].rearrange("p (t m j) -> p m j t", t=PACK, j=PACK)
+            src = raw[a, b][:].rearrange("p j (m t) -> p m j t", t=PACK)
+            return dst, src
+
+        def cast_on_scalar(a, b, l):
+            dst, src = weave_w1(a, b, l)
+            nc.scalar.activation(dst, src, ACT.Copy, scale=1.0 - 2.0 * l)
+
+        def cast_on_vector(a, b):
+            dst, src = weave_w1(a, b, 0)
+            nc.vector.tensor_copy(dst, src)
+
+        def negate_on_vector(a, b):
+            w_bf[a, b, 1] = keep.tile([P, PACK * PASS], BF16, name=f"w_bf{a}{b}1", tag=f"w_bf{a}{b}1", align_bytes=64)
+            nc.vector.tensor_scalar(w_bf[a, b, 1][:], w_bf[a, b, 0][:], -1.0, None, ALU.mult)
+
+        w_codes = {}
+        w_sc = {}
+
+        def quantise_w1(a, b):
+            for l in range(2):
+                src = w_bf[a, b, l]
+                w_codes[a, b, l] = keep.tile([P, PASS], U32, name=f"w_codes{a}{b}{l}", align_bytes=64)
+                w_sc[a, b, l] = keep.tile([P, PASS], U8, name=f"w_sc{a}{b}{l}", align_bytes=64)
+                nc.vector.quantize_mx(out=w_codes[a, b, l][:].bitcast(FP8X4), scales=w_sc[a, b, l][:], in_=src[:])
+
+        got = {}
+        got_tiles = {0: keep.tile([P, 4 * HALF], U16, name="got_first", align_bytes=64)}
+
+        def gather_words(a, h):
+            for l in range(2):
+                first = (2 * a + l) * HALF
+                got[a, l, h] = got_tiles[h][:, first : first + HALF]
+                offsets = lists[l][:, h * HALF // 16 : (h + 1) * HALF // 16]
+                nc.vector.tensor_copy(got[a, l, h], tab_w[a][:].indirect(offsets))
+
+        cast_on_scalar(0, 0, 0)
+        for a in range(2):
+            shift = 24 + 4 * a
+            nc.sync.dma_start(
+                out=planes[0 : P - shift, 2 * S * a : 2 * S * (a + 1)].bitcast(I32),
+                in_=sc_got[shift:P, :].bitcast(I32),
+            )
+        load_w1(0, 1, "tab_sc")
+        load_w1(1, 1, "raw0")
+        cast_on_scalar(1, 0, 0)
+        cast_on_scalar(1, 0, 1)
+
+        w2_w = keep.tile([P, 2, 2 * N], U8, name="w2_w", tag="raw1", align_bytes=64)
+        w2_sc = keep.tile([P, 2, N], U8, name="w2_sc", tag="sc_got", align_bytes=64)
+        nc.gpsimd.memset(w2_sc[:].bitcast(I32), 0)
+        nc.sync.dma_start(out=w2_w[:].bitcast(I32), in_=w2_words.rearrange("a p c -> p a c").bitcast(I32))
+        for q in range(4):
+            nc.sync.dma_start(
+                out=w2_sc[32 * q : 32 * q + 4, :, :].bitcast(I32),
+                in_=w2_scales[:, 4 * q : 4 * q + 4, :].rearrange("a r c -> r a c").bitcast(I32),
+            )
+
+        negate_on_vector(0, 0)
+        quantise_w1(0, 0)
+        gather_words(0, 0)
+        gather_words(1, 0)
+        quantise_w1(1, 0)
+        cast_on_scalar(0, 1, 0)
+        got_tiles[1] = keep.tile([P, 4 * HALF], U16, name="got_second", tag="w_bf101", align_bytes=64)
+        gather_words(0, 1)
+        gather_words(1, 1)
+        negate_on_vector(0, 1)
+        quantise_w1(0, 1)
+        cast_on_vector(1, 1)
+        negate_on_vector(1, 1)
+        quantise_w1(1, 1)
+
+        h_codes = {}
+        h_sc = {}
+
+        def distances(b, h):
+            diffs = [psum.tile([P, HALF], F32, name="diff", tag="bank", bufs=6) for t in range(PACK)]
+            for a in range(2):
+                for t in range(PACK):
+                    cols = slice(t * P, (t + 1) * P)
+                    for l in range(2):
+                        nc.tensor.matmul_mx(
+                            out=diffs[t][:],
+                            lhsT=w_codes[a, b, l][:, cols].bitcast(FP8X4),
+                            lhsT_scale=w_sc[a, b, l][:, cols],
+                            rhs=got[a, l, h].bitcast(FP4X4),
+                            rhs_scale=planes[:, (2 * a + l) * S + h * HALF : (2 * a + l) * S + (h + 1) * HALF],
+                            start=(a == 0 and l == 0),
+                            stop=(a == 1 and l == 1),
+                        )
+            return diffs
+
+        def absolute(diff, on_vector):
+            dist = work.tile([P, HALF], F32, name="dist", bufs=5)
+            if on_vector:
+                flipped = work.tile([P, HALF], F32, name="flipped")
+                nc.vector.tensor_scalar(flipped[:], diff[:], -1.0, None, ALU.mult)
+                nc.vector.tensor_tensor(dist[:], diff[:], flipped[:], ALU.max)
+            else:
+                nc.scalar.activation(dist[:], diff[:], ACT.Abs)
+            return dist
+
+        def fade_out(like, dist, b, t, cols):
+            col = slice(PACK * b + t, PACK * b + t + 1)
+            nc.scalar.activation(like[:, t, :], dist[:, cols], ACT.Exp, bias=ln_gain[:, col], scale=neg_fade[:, col])
+
+        def quantise_h(like, key, width):
+            woven = work.tile([P, width * PACK], BF16, name="woven", align_bytes=64)
+            nc.vector.tensor_copy(
+                woven[:].rearrange("p (c i t) -> p c t i", i=4, t=PACK),
+                like[:].rearrange("p t (c i) -> p c t i", i=4),
+            )
+            h_codes[key] = keep.tile([P, width], U32, name="h_codes%d%d%d" % key, align_bytes=64)
+            h_sc[key] = keep.tile([P, width], U8, name="h_sc%d%d%d" % key, align_bytes=64)
+            nc.vector.quantize_mx(out=h_codes[key][:].bitcast(FP8X4), scales=h_sc[key][:], in_=woven[:])
+
+        def likeness(b, h, vector_tiles):
+            diffs = distances(b, h)
+            like = keep.tile([P, PACK, HALF], BF16, name=f"like{b}{h}", align_bytes=64)
+            for t in range(PACK):
+                dist = absolute(diffs[t], t in vector_tiles)
+                fade_out(like, dist, b, t, slice(0, HALF))
+            quantise_h(like, (b, h, 0), HALF)
+
+        def factor_pass(acc, n, key, cols, start, stop):
+            b = key[0]
+            nc.tensor.matmul_mx(
+                out=acc,
+                lhsT=w2_w[:, b, 2 * P * n : 2 * P * (n + 1)].bitcast(FP4X4),
+                lhsT_scale=w2_sc[:, b, P * n : P * (n + 1)],
+                rhs=h_codes[key][:, cols].bitcast(FP8X4),
+                rhs_scale=h_sc[key][:, cols],
+                start=start,
+                stop=stop,
+            )
+
+        likeness(0, 0, ())
+        likeness(0, 1, ())
+        likeness(1, 0, ())
+        diffs = distances(1, 1)
+        dists = [absolute(diffs[t], False) for t in range(PACK)]
+
+        for n in range(2):
+            acc = psum.tile([P, HALF], F32, name="acc", tag="acc", bufs=2)
+            for b in range(2):
+                factor_pass(acc[:], n, (b, 0, 0), slice(0, HALF), b == 0, b == 1)
+            res = keep.tile([P, HALF], F32, name=f"res{n}")
+            nc.vector.tensor_copy(res[:], acc[:])
+            nc.sync.dma_start(out=out[P * n : P * (n + 1), 0:HALF], in_=res[:])
+
+        QUARTER = HALF // 2
+        for u in range(2):
+            cols = slice(u * QUARTER, (u + 1) * QUARTER)
+            like = keep.tile([P, PACK, QUARTER], BF16, name=f"like_end{u}", align_bytes=64)
+            for t in range(PACK):
+                fade_out(like, dists[t], 1, t, cols)
+            quantise_h(like, (1, 1, u), QUARTER)
+            for n in range(2):
+                if u == 0:
+                    acc = psum.tile([P, HALF], F32, name="acc", tag="bank", bufs=6)
+                else:
+                    acc = psum.tile([P, HALF], F32, name="acc", tag="acc", bufs=2)
+                for c in range(2):
+                    first = u * QUARTER + c * P
+                    factor_pass(acc[:, c * P : (c + 1) * P], n, (0, 1, 0), slice(first, first + P), c == 0, False)
+                for c in range(2):
+                    factor_pass(acc[:, c * P : (c + 1) * P], n, (1, 1, u), slice(c * P, (c + 1) * P), False, c == 1)
+                res = keep.tile([P, QUARTER], F32, name=f"res_end{u}{n}")
+                if n == 0 or u == 0:
+                    nc.vector.tensor_copy(res[:], acc[:, 0:QUARTER])
+                else:
+                    nc.scalar.copy(res[:], acc[:, 0:QUARTER])
+                first = HALF + u * QUARTER
+                nc.sync.dma_start(out=out[P * n : P * (n + 1), first : first + QUARTER], in_=res[:])

@@ -21,6 +21,7 @@ PACK = 4
 PASS = P * PACK
 HALF = 512
 LN_RANGE = 2.0**64
+SHIFT = (48, -8)
 
 
 def tile_list_friendship_homophily_kernel(
@@ -32,79 +33,99 @@ def tile_list_friendship_homophily_kernel(
         work = ctx.enter_context(tc.tile_pool(name="work", bufs=2))
         psum = ctx.enter_context(tc.psum_pool(name="psum", bufs=1))
 
+        fade_t = keep.tile([P, 2, PACK], F32, name="fade_t")
+        gain_t = keep.tile([P, 2, PACK], F32, name="gain_t")
+        nc.sync.dma_start(out=gain_t[:], in_=gain.rearrange("(b p t) -> p b t", b=2, t=PACK))
+
         lists = []
         for name, src in (("pupils", offs), ("friends", offs2)):
             tile = keep.tile([P, S // 16], U16, name=name)
             nc.sync.dma_start(tile[:], src)
             lists.append(tile)
 
-        fade_t = keep.tile([P, 2, PACK], F32, name="fade_t")
-        gain_t = keep.tile([P, 2, PACK], F32, name="gain_t")
-        nc.sync.dma_start(out=gain_t[:], in_=gain.rearrange("(b p t) -> p b t", b=2, t=PACK))
-
         tab_sc = keep.tile([P, T], U8, name="tab_sc", tag="tab_sc", align_bytes=64)
+        for first, last in ((0, 48), (64, 80), (96, 128)):
+            nc.vector.memset(tab_sc[first:last, :].bitcast(I32), 0)
         for q in range(4):
-            nc.vector.memset(tab_sc[32 * q : 32 * q + 24, :].bitcast(I32), 0)
+            first = 32 * q + SHIFT[q // 2]
             nc.sync.dma_start(
-                out=tab_sc[32 * q + 24 : 32 * q + 32, :].bitcast(I32),
+                out=tab_sc[first : first + 8, :].bitcast(I32),
                 in_=tab_scales[:, 4 * q : 4 * q + 4, :].bitcast(I32),
             )
 
 
         raw = {}
 
-        def load_w1(a, b, slot):
-            raw[a, b] = keep.tile([P, PACK, PASS], F32, name=f"raw{a}{b}", tag=slot, align_bytes=64)
-            rows = w1[a * PASS : (a + 1) * PASS, b * PASS : (b + 1) * PASS]
-            nc.sync.dma_start(out=raw[a, b][:], in_=rows.rearrange("(p j) c -> p j c", j=PACK))
+        def load_w1(a, b, slots):
+            rows = w1[a * PASS : (a + 1) * PASS, b * PASS : (b + 1) * PASS].rearrange("(p j) c -> p j c", j=PACK)
+            width = PASS // len(slots)
+            for i, slot in enumerate(slots):
+                piece = keep.tile([P, PACK, width], F32, name=f"raw{a}{b}{i}", tag=slot, align_bytes=64)
+                nc.sync.dma_start(out=piece[:], in_=rows[:, :, i * width : (i + 1) * width])
+                raw.setdefault((a, b), []).append(piece)
 
-        load_w1(0, 0, "raw0")
-        nc.sync.dma_start(out=fade_t[:], in_=fade.rearrange("(b p t) -> p b t", b=2, t=PACK))
-        load_w1(1, 0, "raw1")
+        load_w1(0, 0, ["raw00"])
+        nc.gpsimd.dma_start(out=fade_t[:], in_=fade.rearrange("(b p t) -> p b t", b=2, t=PACK))
+        load_w1(1, 0, ["raw10"])
         tab_w = []
         for a in range(2):
             tile = keep.tile([P, T], U16, name=f"tab_w{a}", align_bytes=64)
             nc.sync.dma_start(out=tile[:].bitcast(I32), in_=tab_words[a].bitcast(I32))
             tab_w.append(tile)
 
-        planes = keep.tile([P, 4 * S], U8, name="planes", align_bytes=64)
-        nc.gpsimd.memset(planes[96:128, :].bitcast(I32), 0)
 
         gain_flat = gain_t[:].rearrange("p b t -> p (b t)")
         parts = keep.tile([P, 3, 8], F32, name="parts")
-        nc.vector.tensor_scalar(parts[:, 0, :], gain_flat, 1.0 / LN_RANGE, LN_RANGE, ALU.max, ALU.min)
-        nc.vector.tensor_scalar(parts[:, 1, :], gain_flat, LN_RANGE, 1.0 / LN_RANGE, ALU.max, ALU.mult)
-        nc.vector.tensor_scalar(parts[:, 2, :], gain_flat, 1.0 / LN_RANGE, LN_RANGE, ALU.min, ALU.mult)
+        nc.gpsimd.tensor_scalar(parts[:, 0, :], gain_flat, 1.0 / LN_RANGE, LN_RANGE, ALU.max, ALU.min)
+        nc.gpsimd.tensor_scalar(parts[:, 1, :], gain_flat, LN_RANGE, 1.0 / LN_RANGE, ALU.max, ALU.mult)
+        nc.gpsimd.tensor_scalar(parts[:, 2, :], gain_flat, 1.0 / LN_RANGE, LN_RANGE, ALU.min, ALU.mult)
         ln_parts = keep.tile([P, 3, 8], F32, name="ln_parts")
         nc.scalar.activation(ln_parts[:], parts[:], ACT.Ln)
         warm = keep.tile([P, 1], F32, name="warm")
         nc.scalar.activation(warm[:], ln_parts[:, 1, 0:1], ACT.Exp)
-        ln_two = keep.tile([P, 8], F32, name="ln_two")
         ln_gain = keep.tile([P, 8], F32, name="ln_gain")
-        nc.gpsimd.tensor_tensor(ln_two[:], ln_parts[:, 1, :], ln_parts[:, 2, :], ALU.add)
-        nc.gpsimd.tensor_tensor(ln_gain[:], ln_two[:], ln_parts[:, 0, :], ALU.add)
+        nc.vector.tensor_reduce(ln_gain[:], ln_parts[:].rearrange("p s c -> p c s"), mybir.AxisListType.X, ALU.add)
         neg_fade = keep.tile([P, 8], F32, name="neg_fade")
         nc.gpsimd.tensor_scalar(neg_fade[:], fade_t[:].rearrange("p b t -> p (b t)"), -1.0, 0.0, ALU.mult, ALU.add)
 
-        sc_got = keep.tile([P, 2 * S], U8, name="sc_got", tag="sc_got", align_bytes=64)
-        for l in range(2):
-            nc.vector.tensor_copy(sc_got[:, l * S : (l + 1) * S], tab_sc[:].indirect(lists[l][:]))
+        sc_got = []
+        for h in range(2):
+            tile = keep.tile([P, 2 * HALF], U8, name=f"sc_got{h}", tag=f"sc_got{h}", align_bytes=64)
+            for l in range(2):
+                offsets = lists[l][:, h * HALF // 16 : (h + 1) * HALF // 16]
+                nc.vector.tensor_copy(tile[:, l * HALF : (l + 1) * HALF], tab_sc[:].indirect(offsets))
+            sc_got.append(tile)
+
+        planes = {}
+
+        def move_planes(h, queue):
+            planes[h] = keep.tile([P, 4 * HALF], U8, name=f"planes{h}", tag=("planes0", "w_bf001")[h], align_bytes=64)
+            for a in range(2):
+                for side in range(2):
+                    first = 64 * side + SHIFT[side] + 4 * a
+                    queue.dma_start(
+                        out=planes[h][64 * side : 64 * (side + 1), 2 * HALF * a : 2 * HALF * (a + 1)].bitcast(I32),
+                        in_=sc_got[h][first : first + 64, :].bitcast(I32),
+                    )
 
         w_bf = {}
 
         def weave_w1(a, b, l):
             w_bf[a, b, l] = keep.tile([P, PACK * PASS], BF16, name=f"w_bf{a}{b}{l}", tag=f"w_bf{a}{b}{l}", align_bytes=64)
             dst = w_bf[a, b, l][:].rearrange("p (t m j) -> p m j t", t=PACK, j=PACK)
-            src = raw[a, b][:].rearrange("p j (m t) -> p m j t", t=PACK)
-            return dst, src
+            width = P // len(raw[a, b])
+            return [
+                (dst[:, i * width : (i + 1) * width], piece[:].rearrange("p j (m t) -> p m j t", t=PACK))
+                for i, piece in enumerate(raw[a, b])
+            ]
 
         def cast_on_scalar(a, b, l):
-            dst, src = weave_w1(a, b, l)
-            nc.scalar.activation(dst, src, ACT.Copy, scale=1.0 - 2.0 * l)
+            for dst, src in weave_w1(a, b, l):
+                nc.scalar.activation(dst, src, ACT.Copy, scale=1.0 - 2.0 * l)
 
         def cast_on_vector(a, b):
-            dst, src = weave_w1(a, b, 0)
-            nc.vector.tensor_copy(dst, src)
+            for dst, src in weave_w1(a, b, 0):
+                nc.vector.tensor_copy(dst, src)
 
         def negate_on_vector(a, b):
             w_bf[a, b, 1] = keep.tile([P, PACK * PASS], BF16, name=f"w_bf{a}{b}1", tag=f"w_bf{a}{b}1", align_bytes=64)
@@ -130,21 +151,19 @@ def tile_list_friendship_homophily_kernel(
                 offsets = lists[l][:, h * HALF // 16 : (h + 1) * HALF // 16]
                 nc.vector.tensor_copy(got[a, l, h], tab_w[a][:].indirect(offsets))
 
+        move_planes(0, nc.scalar)
         cast_on_scalar(0, 0, 0)
-        for a in range(2):
-            shift = 24 + 4 * a
-            nc.sync.dma_start(
-                out=planes[0 : P - shift, 2 * S * a : 2 * S * (a + 1)].bitcast(I32),
-                in_=sc_got[shift:P, :].bitcast(I32),
-            )
-        load_w1(0, 1, "tab_sc")
-        load_w1(1, 1, "raw0")
+        load_w1(0, 1, ["raw01", "raw00"])
         cast_on_scalar(1, 0, 0)
         cast_on_scalar(1, 0, 1)
 
-        w2_w = keep.tile([P, 2, 2 * N], U8, name="w2_w", tag="raw1", align_bytes=64)
-        w2_sc = keep.tile([P, 2, N], U8, name="w2_sc", tag="sc_got", align_bytes=64)
-        nc.gpsimd.memset(w2_sc[:].bitcast(I32), 0)
+        negate_on_vector(0, 0)
+        quantise_w1(0, 0)
+        load_w1(1, 1, ["w_bf000"])
+        move_planes(1, nc.sync)
+        w2_w = keep.tile([P, 2, 2 * N], U8, name="w2_w", tag="raw10", align_bytes=64)
+        w2_sc = keep.tile([P, 2, N], U8, name="w2_sc", tag="sc_got1", align_bytes=64)
+        nc.vector.memset(w2_sc[:].bitcast(I32), 0)
         nc.sync.dma_start(out=w2_w[:].bitcast(I32), in_=w2_words.rearrange("a p c -> p a c").bitcast(I32))
         for q in range(4):
             nc.sync.dma_start(
@@ -152,8 +171,6 @@ def tile_list_friendship_homophily_kernel(
                 in_=w2_scales[:, 4 * q : 4 * q + 4, :].rearrange("a r c -> r a c").bitcast(I32),
             )
 
-        negate_on_vector(0, 0)
-        quantise_w1(0, 0)
         gather_words(0, 0)
         gather_words(1, 0)
         quantise_w1(1, 0)
@@ -168,6 +185,7 @@ def tile_list_friendship_homophily_kernel(
         quantise_w1(1, 1)
 
         h_codes = {}
+        likes = {}
         h_sc = {}
 
         def distances(b, h):
@@ -181,7 +199,7 @@ def tile_list_friendship_homophily_kernel(
                             lhsT=w_codes[a, b, l][:, cols].bitcast(FP8X4),
                             lhsT_scale=w_sc[a, b, l][:, cols],
                             rhs=got[a, l, h].bitcast(FP4X4),
-                            rhs_scale=planes[:, (2 * a + l) * S + h * HALF : (2 * a + l) * S + (h + 1) * HALF],
+                            rhs_scale=planes[h][:, (2 * a + l) * HALF : (2 * a + l + 1) * HALF],
                             start=(a == 0 and l == 0),
                             stop=(a == 1 and l == 1),
                         )
@@ -214,6 +232,7 @@ def tile_list_friendship_homophily_kernel(
         def likeness(b, h, vector_tiles):
             diffs = distances(b, h)
             like = keep.tile([P, PACK, HALF], BF16, name=f"like{b}{h}", align_bytes=64)
+            likes[b, h] = like
             for t in range(PACK):
                 dist = absolute(diffs[t], t in vector_tiles)
                 fade_out(like, dist, b, t, slice(0, HALF))

@@ -21,7 +21,7 @@ PACK = 4
 PASS = P * PACK
 HALF = 512
 LN_RANGE = 2.0**64
-SHIFT = (48, -8)
+SCALE_HOME = 48
 
 
 def tile_list_friendship_homophily_kernel(
@@ -34,7 +34,7 @@ def tile_list_friendship_homophily_kernel(
         psum = ctx.enter_context(tc.psum_pool(name="psum", bufs=1))
 
         fade_t = keep.tile([P, 2, PACK], F32, name="fade_t")
-        gain_t = keep.tile([P, 2, PACK], F32, name="gain_t")
+        gain_t = keep.tile([P, 2, PACK], F32, name="gain_t", tag="sc_got0", align_bytes=64)
         nc.sync.dma_start(out=gain_t[:], in_=gain.rearrange("(b p t) -> p b t", b=2, t=PACK))
 
         lists = []
@@ -46,12 +46,11 @@ def tile_list_friendship_homophily_kernel(
         tab_sc = keep.tile([P, T], U8, name="tab_sc", tag="tab_sc", align_bytes=64)
         for first, last in ((0, 48), (64, 80), (96, 128)):
             nc.vector.memset(tab_sc[first:last, :].bitcast(I32), 0)
-        for q in range(4):
-            first = 32 * q + SHIFT[q // 2]
-            nc.sync.dma_start(
-                out=tab_sc[first : first + 8, :].bitcast(I32),
-                in_=tab_scales[:, 4 * q : 4 * q + 4, :].bitcast(I32),
-            )
+        scale_rows = tab_scales.rearrange("a (side odd r) t -> odd (a side) r t", side=2, odd=2)
+        for odd in range(2):
+            first = SCALE_HOME + 32 * odd
+            nc.sync.dma_start(out=tab_sc[first : first + 16, :].bitcast(I32), in_=scale_rows[odd].bitcast(I32))
+        nc.sync.dma_start(out=fade_t[:], in_=fade.rearrange("(b p t) -> p b t", b=2, t=PACK))
 
 
         raw = {}
@@ -65,7 +64,6 @@ def tile_list_friendship_homophily_kernel(
                 raw.setdefault((a, b), []).append(piece)
 
         load_w1(0, 0, ["raw00"])
-        nc.gpsimd.dma_start(out=fade_t[:], in_=fade.rearrange("(b p t) -> p b t", b=2, t=PACK))
         load_w1(1, 0, ["raw10"])
         tab_w = []
         for a in range(2):
@@ -76,9 +74,9 @@ def tile_list_friendship_homophily_kernel(
 
         gain_flat = gain_t[:].rearrange("p b t -> p (b t)")
         parts = keep.tile([P, 3, 8], F32, name="parts")
-        nc.gpsimd.tensor_scalar(parts[:, 0, :], gain_flat, 1.0 / LN_RANGE, LN_RANGE, ALU.max, ALU.min)
-        nc.gpsimd.tensor_scalar(parts[:, 1, :], gain_flat, LN_RANGE, 1.0 / LN_RANGE, ALU.max, ALU.mult)
-        nc.gpsimd.tensor_scalar(parts[:, 2, :], gain_flat, 1.0 / LN_RANGE, LN_RANGE, ALU.min, ALU.mult)
+        nc.vector.tensor_scalar(parts[:, 0, :], gain_flat, 1.0 / LN_RANGE, LN_RANGE, ALU.max, ALU.min)
+        nc.vector.tensor_scalar(parts[:, 1, :], gain_flat, LN_RANGE, 1.0 / LN_RANGE, ALU.max, ALU.mult)
+        nc.vector.tensor_scalar(parts[:, 2, :], gain_flat, 1.0 / LN_RANGE, LN_RANGE, ALU.min, ALU.mult)
         ln_parts = keep.tile([P, 3, 8], F32, name="ln_parts")
         nc.scalar.activation(ln_parts[:], parts[:], ACT.Ln)
         warm = keep.tile([P, 1], F32, name="warm")
@@ -86,7 +84,7 @@ def tile_list_friendship_homophily_kernel(
         ln_gain = keep.tile([P, 8], F32, name="ln_gain")
         nc.vector.tensor_reduce(ln_gain[:], ln_parts[:].rearrange("p s c -> p c s"), mybir.AxisListType.X, ALU.add)
         neg_fade = keep.tile([P, 8], F32, name="neg_fade")
-        nc.gpsimd.tensor_scalar(neg_fade[:], fade_t[:].rearrange("p b t -> p (b t)"), -1.0, 0.0, ALU.mult, ALU.add)
+        nc.vector.tensor_scalar(neg_fade[:], fade_t[:].rearrange("p b t -> p (b t)"), -1.0, None, ALU.mult)
 
         sc_got = []
         for h in range(2):
@@ -99,10 +97,10 @@ def tile_list_friendship_homophily_kernel(
         planes = {}
 
         def move_planes(h, queue):
-            planes[h] = keep.tile([P, 4 * HALF], U8, name=f"planes{h}", tag=("planes0", "w_bf001")[h], align_bytes=64)
+            planes[h] = keep.tile([P, 4 * HALF], U8, name=f"planes{h}", tag=("raw00", "w_bf001")[h], align_bytes=64)
             for a in range(2):
                 for side in range(2):
-                    first = 64 * side + SHIFT[side] + 4 * a
+                    first = SCALE_HOME + 8 * a + 4 * side
                     queue.dma_start(
                         out=planes[h][64 * side : 64 * (side + 1), 2 * HALF * a : 2 * HALF * (a + 1)].bitcast(I32),
                         in_=sc_got[h][first : first + 64, :].bitcast(I32),
@@ -134,12 +132,12 @@ def tile_list_friendship_homophily_kernel(
         w_codes = {}
         w_sc = {}
 
-        def quantise_w1(a, b):
-            for l in range(2):
-                src = w_bf[a, b, l]
-                w_codes[a, b, l] = keep.tile([P, PASS], U32, name=f"w_codes{a}{b}{l}", align_bytes=64)
-                w_sc[a, b, l] = keep.tile([P, PASS], U8, name=f"w_sc{a}{b}{l}", align_bytes=64)
-                nc.vector.quantize_mx(out=w_codes[a, b, l][:].bitcast(FP8X4), scales=w_sc[a, b, l][:], in_=src[:])
+        def quantise_w1(a, b, l):
+            w_codes[a, b, l] = keep.tile([P, PASS], U32, name=f"w_codes{a}{b}{l}", align_bytes=64)
+            w_sc[a, b, l] = keep.tile([P, PASS], U8, name=f"w_sc{a}{b}{l}", align_bytes=64)
+            nc.vector.quantize_mx(
+                out=w_codes[a, b, l][:].bitcast(FP8X4), scales=w_sc[a, b, l][:], in_=w_bf[a, b, l][:]
+            )
 
         got = {}
         got_tiles = {0: keep.tile([P, 4 * HALF], U16, name="got_first", align_bytes=64)}
@@ -151,14 +149,15 @@ def tile_list_friendship_homophily_kernel(
                 offsets = lists[l][:, h * HALF // 16 : (h + 1) * HALF // 16]
                 nc.vector.tensor_copy(got[a, l, h], tab_w[a][:].indirect(offsets))
 
-        move_planes(0, nc.scalar)
+        load_w1(0, 1, ["raw01", "raw01_rest"])
         cast_on_scalar(0, 0, 0)
-        load_w1(0, 1, ["raw01", "raw00"])
+        move_planes(0, nc.scalar)
         cast_on_scalar(1, 0, 0)
         cast_on_scalar(1, 0, 1)
 
         negate_on_vector(0, 0)
-        quantise_w1(0, 0)
+        quantise_w1(0, 0, 0)
+        quantise_w1(0, 0, 1)
         load_w1(1, 1, ["w_bf000"])
         move_planes(1, nc.sync)
         w2_w = keep.tile([P, 2, 2 * N], U8, name="w2_w", tag="raw10", align_bytes=64)
@@ -172,20 +171,22 @@ def tile_list_friendship_homophily_kernel(
             )
 
         gather_words(0, 0)
+        quantise_w1(1, 0, 0)
         gather_words(1, 0)
-        quantise_w1(1, 0)
+        quantise_w1(1, 0, 1)
         cast_on_scalar(0, 1, 0)
         got_tiles[1] = keep.tile([P, 4 * HALF], U16, name="got_second", tag="w_bf101", align_bytes=64)
         gather_words(0, 1)
         gather_words(1, 1)
         negate_on_vector(0, 1)
-        quantise_w1(0, 1)
         cast_on_vector(1, 1)
+        quantise_w1(0, 1, 0)
         negate_on_vector(1, 1)
-        quantise_w1(1, 1)
+        quantise_w1(0, 1, 1)
+        quantise_w1(1, 1, 0)
+        quantise_w1(1, 1, 1)
 
         h_codes = {}
-        likes = {}
         h_sc = {}
 
         def distances(b, h):
@@ -205,14 +206,9 @@ def tile_list_friendship_homophily_kernel(
                         )
             return diffs
 
-        def absolute(diff, on_vector):
-            dist = work.tile([P, HALF], F32, name="dist", bufs=5)
-            if on_vector:
-                flipped = work.tile([P, HALF], F32, name="flipped")
-                nc.vector.tensor_scalar(flipped[:], diff[:], -1.0, None, ALU.mult)
-                nc.vector.tensor_tensor(dist[:], diff[:], flipped[:], ALU.max)
-            else:
-                nc.scalar.activation(dist[:], diff[:], ACT.Abs)
+        def absolute(diff):
+            dist = work.tile([P, HALF], F32, name="dist", bufs=6)
+            nc.scalar.activation(dist[:], diff[:], ACT.Abs)
             return dist
 
         def fade_out(like, dist, b, t, cols):
@@ -229,15 +225,6 @@ def tile_list_friendship_homophily_kernel(
             h_sc[key] = keep.tile([P, width], U8, name="h_sc%d%d%d" % key, align_bytes=64)
             nc.vector.quantize_mx(out=h_codes[key][:].bitcast(FP8X4), scales=h_sc[key][:], in_=woven[:])
 
-        def likeness(b, h, vector_tiles):
-            diffs = distances(b, h)
-            like = keep.tile([P, PACK, HALF], BF16, name=f"like{b}{h}", align_bytes=64)
-            likes[b, h] = like
-            for t in range(PACK):
-                dist = absolute(diffs[t], t in vector_tiles)
-                fade_out(like, dist, b, t, slice(0, HALF))
-            quantise_h(like, (b, h, 0), HALF)
-
         def factor_pass(acc, n, key, cols, start, stop):
             b = key[0]
             nc.tensor.matmul_mx(
@@ -250,11 +237,31 @@ def tile_list_friendship_homophily_kernel(
                 stop=stop,
             )
 
-        likeness(0, 0, ())
-        likeness(0, 1, ())
-        likeness(1, 0, ())
-        diffs = distances(1, 1)
-        dists = [absolute(diffs[t], False) for t in range(PACK)]
+        QUARTER = HALF // 2
+        waiting = []
+
+        def finish_waiting():
+            like, dist, key, t, width = waiting.pop()
+            fade_out(like, dist, key[0], t, slice(0, width))
+            if t == PACK - 1:
+                quantise_h(like, key, width)
+
+        for b in range(2):
+            for h in range(2):
+                width = QUARTER if b == 1 and h == 1 else HALF
+                diffs = distances(b, h)
+                like = keep.tile([P, PACK, width], BF16, name=f"like{b}{h}", align_bytes=64)
+                dists = []
+                for t in range(PACK):
+                    dists.append(absolute(diffs[t]))
+                    if waiting:
+                        finish_waiting()
+                    waiting.append((like, dists[t], (b, h, 0), t, width))
+        finish_waiting()
+        like = keep.tile([P, PACK, QUARTER], BF16, name="like_last", align_bytes=64)
+        for t in range(PACK):
+            fade_out(like, dists[t], 1, t, slice(QUARTER, HALF))
+        quantise_h(like, (1, 1, 1), QUARTER)
 
         for n in range(2):
             acc = psum.tile([P, HALF], F32, name="acc", tag="acc", bufs=2)
@@ -264,13 +271,7 @@ def tile_list_friendship_homophily_kernel(
             nc.vector.tensor_copy(res[:], acc[:])
             nc.sync.dma_start(out=out[P * n : P * (n + 1), 0:HALF], in_=res[:])
 
-        QUARTER = HALF // 2
         for u in range(2):
-            cols = slice(u * QUARTER, (u + 1) * QUARTER)
-            like = keep.tile([P, PACK, QUARTER], BF16, name=f"like_end{u}", align_bytes=64)
-            for t in range(PACK):
-                fade_out(like, dists[t], 1, t, cols)
-            quantise_h(like, (1, 1, u), QUARTER)
             for n in range(2):
                 if u == 0:
                     acc = psum.tile([P, HALF], F32, name="acc", tag="bank", bufs=6)

from contextlib import ExitStack

import concourse.mybir as mybir

K, H, N, T, S = 1024, 1024, 256, 4096, 1024
FLOPS = 2 * K * H * S * 2 + 2 * H * N * S

F32 = mybir.dt.float32
BF16 = mybir.dt.bfloat16
I32 = mybir.dt.int32
U32 = mybir.dt.uint32
U16 = mybir.dt.uint16
U8 = mybir.dt.uint8
FP8X4 = mybir.dt.float8_e4m3fn_x4
FP4X4 = mybir.dt.float4_e2m1fn_x4
ALU = mybir.AluOpType
ACT = mybir.ActivationFunctionType

P = 128
PACK = 4
PASS = P * PACK
HALF = 512
LN_RANGE = 2.0**64
SCALE_HOME = 48


def tile_list_friendship_homophily_kernel(
    tc, tab_words, tab_scales, offs, offs2, w1, fade, gain, w2_words, w2_scales, out
):
    nc = tc.nc
    with ExitStack() as ctx:
        keep = ctx.enter_context(tc.tile_pool(name="keep", bufs=1))
        work = ctx.enter_context(tc.tile_pool(name="work", bufs=2))
        psum = ctx.enter_context(tc.psum_pool(name="psum", bufs=1))

        fade_t = keep.tile([P, 2, PACK], F32, name="fade_t")
        gain_t = keep.tile([P, 2, PACK], F32, name="gain_t", tag="sc_got0", align_bytes=64)
        nc.sync.dma_start(out=gain_t[:], in_=gain.rearrange("(b p t) -> p b t", b=2, t=PACK))

        lists = []
        for name, src in (("pupils", offs), ("friends", offs2)):
            tile = keep.tile([P, S // 16], U16, name=name)
            nc.sync.dma_start(tile[:], src)
            lists.append(tile)

        tab_sc = keep.tile([P, T], U8, name="tab_sc", tag="tab_sc", align_bytes=64)
        for first, last in ((0, 48), (64, 80), (96, 128)):
            nc.vector.memset(tab_sc[first:last, :].bitcast(I32), 0)
        scale_rows = tab_scales.rearrange("a (side odd r) t -> odd (a side) r t", side=2, odd=2)
        for odd in range(2):
            first = SCALE_HOME + 32 * odd
            nc.sync.dma_start(out=tab_sc[first : first + 16, :].bitcast(I32), in_=scale_rows[odd].bitcast(I32))
        nc.sync.dma_start(out=fade_t[:], in_=fade.rearrange("(b p t) -> p b t", b=2, t=PACK))


        raw = {}

        def load_w1(a, b, slots):
            rows = w1[a * PASS : (a + 1) * PASS, b * PASS : (b + 1) * PASS].rearrange("(p j) c -> p j c", j=PACK)
            width = PASS // len(slots)
            for i, slot in enumerate(slots):
                piece = keep.tile([P, PACK, width], F32, name=f"raw{a}{b}{i}", tag=slot, align_bytes=64)
                nc.sync.dma_start(out=piece[:], in_=rows[:, :, i * width : (i + 1) * width])
                raw.setdefault((a, b), []).append(piece)

        load_w1(0, 0, ["raw00"])
        load_w1(1, 0, ["raw10"])
        tab_w = []
        for a in range(2):
            tile = keep.tile([P, T], U16, name=f"tab_w{a}", align_bytes=64)
            nc.sync.dma_start(out=tile[:].bitcast(I32), in_=tab_words[a].bitcast(I32))
            tab_w.append(tile)


        gain_flat = gain_t[:].rearrange("p b t -> p (b t)")
        parts = keep.tile([P, 3, 8], F32, name="parts")
        nc.vector.tensor_scalar(parts[:, 0, :], gain_flat, 1.0 / LN_RANGE, LN_RANGE, ALU.max, ALU.min)
        nc.vector.tensor_scalar(parts[:, 1, :], gain_flat, LN_RANGE, 1.0 / LN_RANGE, ALU.max, ALU.mult)
        nc.vector.tensor_scalar(parts[:, 2, :], gain_flat, 1.0 / LN_RANGE, LN_RANGE, ALU.min, ALU.mult)
        ln_parts = keep.tile([P, 3, 8], F32, name="ln_parts")
        nc.scalar.activation(ln_parts[:], parts[:], ACT.Ln)
        warm = keep.tile([P, 1], F32, name="warm")
        nc.scalar.activation(warm[:], ln_parts[:, 1, 0:1], ACT.Exp)
        ln_gain = keep.tile([P, 8], F32, name="ln_gain")
        nc.vector.tensor_reduce(ln_gain[:], ln_parts[:].rearrange("p s c -> p c s"), mybir.AxisListType.X, ALU.add)
        neg_fade = keep.tile([P, 8], F32, name="neg_fade")
        nc.vector.tensor_scalar(neg_fade[:], fade_t[:].rearrange("p b t -> p (b t)"), -1.0, None, ALU.mult)

        sc_got = []
        for h in range(2):
            tile = keep.tile([P, 2 * HALF], U8, name=f"sc_got{h}", tag=f"sc_got{h}", align_bytes=64)
            for l in range(2):
                offsets = lists[l][:, h * HALF // 16 : (h + 1) * HALF // 16]
                nc.vector.tensor_copy(tile[:, l * HALF : (l + 1) * HALF], tab_sc[:].indirect(offsets))
            sc_got.append(tile)

        planes = {}

        def move_planes(h, queue):
            planes[h] = keep.tile([P, 4 * HALF], U8, name=f"planes{h}", tag=("raw00", "w_bf001")[h], align_bytes=64)
            for a in range(2):
                for side in range(2):
                    first = SCALE_HOME + 8 * a + 4 * side
                    queue.dma_start(
                        out=planes[h][64 * side : 64 * (side + 1), 2 * HALF * a : 2 * HALF * (a + 1)].bitcast(I32),
                        in_=sc_got[h][first : first + 64, :].bitcast(I32),
                    )

        w_bf = {}

        def weave_w1(a, b, l):
            w_bf[a, b, l] = keep.tile([P, PACK * PASS], BF16, name=f"w_bf{a}{b}{l}", tag=f"w_bf{a}{b}{l}", align_bytes=64)
            dst = w_bf[a, b, l][:].rearrange("p (t m j) -> p m j t", t=PACK, j=PACK)
            width = P // len(raw[a, b])
            return [
                (dst[:, i * width : (i + 1) * width], piece[:].rearrange("p j (m t) -> p m j t", t=PACK))
                for i, piece in enumerate(raw[a, b])
            ]

        def cast_on_scalar(a, b, l):
            for dst, src in weave_w1(a, b, l):
                nc.scalar.activation(dst, src, ACT.Copy, scale=1.0 - 2.0 * l)

        def cast_on_vector(a, b):
            for dst, src in weave_w1(a, b, 0):
                nc.vector.tensor_copy(dst, src)

        def negate_on_vector(a, b):
            w_bf[a, b, 1] = keep.tile([P, PACK * PASS], BF16, name=f"w_bf{a}{b}1", tag=f"w_bf{a}{b}1", align_bytes=64)
            nc.vector.tensor_scalar(w_bf[a, b, 1][:], w_bf[a, b, 0][:], -1.0, None, ALU.mult)

        w_codes = {}
        w_sc = {}

        def quantise_w1(a, b, l):
            w_codes[a, b, l] = keep.tile([P, PASS], U32, name=f"w_codes{a}{b}{l}", align_bytes=64)
            w_sc[a, b, l] = keep.tile([P, PASS], U8, name=f"w_sc{a}{b}{l}", align_bytes=64)
            nc.vector.quantize_mx(
                out=w_codes[a, b, l][:].bitcast(FP8X4), scales=w_sc[a, b, l][:], in_=w_bf[a, b, l][:]
            )

        got = {}
        got_tiles = {0: keep.tile([P, 4 * HALF], U16, name="got_first", align_bytes=64)}

        def gather_words(a, h):
            for l in range(2):
                first = (2 * a + l) * HALF
                got[a, l, h] = got_tiles[h][:, first : first + HALF]
                offsets = lists[l][:, h * HALF // 16 : (h + 1) * HALF // 16]
                nc.vector.tensor_copy(got[a, l, h], tab_w[a][:].indirect(offsets))

        load_w1(0, 1, ["raw01", "raw01_rest"])
        cast_on_scalar(0, 0, 0)
        move_planes(0, nc.scalar)
        cast_on_scalar(1, 0, 0)
        cast_on_scalar(1, 0, 1)

        negate_on_vector(0, 0)
        quantise_w1(0, 0, 0)
        quantise_w1(0, 0, 1)
        load_w1(1, 1, ["w_bf000"])
        move_planes(1, nc.sync)
        w2_w = keep.tile([P, 2, 2 * N], U8, name="w2_w", tag="raw10", align_bytes=64)
        w2_sc = keep.tile([P, 2, N], U8, name="w2_sc", tag="sc_got1", align_bytes=64)
        nc.vector.memset(w2_sc[:].bitcast(I32), 0)
        nc.sync.dma_start(out=w2_w[:].bitcast(I32), in_=w2_words.rearrange("a p c -> p a c").bitcast(I32))
        for q in range(4):
            nc.sync.dma_start(
                out=w2_sc[32 * q : 32 * q + 4, :, :].bitcast(I32),
                in_=w2_scales[:, 4 * q : 4 * q + 4, :].rearrange("a r c -> r a c").bitcast(I32),
            )

        gather_words(0, 0)
        quantise_w1(1, 0, 0)
        gather_words(1, 0)
        quantise_w1(1, 0, 1)
        cast_on_scalar(0, 1, 0)
        got_tiles[1] = keep.tile([P, 4 * HALF], U16, name="got_second", tag="w_bf101", align_bytes=64)
        gather_words(0, 1)
        gather_words(1, 1)
        negate_on_vector(0, 1)
        cast_on_vector(1, 1)
        quantise_w1(0, 1, 0)
        negate_on_vector(1, 1)
        quantise_w1(0, 1, 1)
        quantise_w1(1, 1, 0)
        quantise_w1(1, 1, 1)

        h_codes = {}
        h_sc = {}

        def distances(b, h):
            diffs = [psum.tile([P, HALF], F32, name="diff", tag="bank", bufs=6) for t in range(PACK)]
            for a in range(2):
                for t in range(PACK):
                    cols = slice(t * P, (t + 1) * P)
                    for l in range(2):
                        nc.tensor.matmul_mx(
                            out=diffs[t][:],
                            lhsT=w_codes[a, b, l][:, cols].bitcast(FP8X4),
                            lhsT_scale=w_sc[a, b, l][:, cols],
                            rhs=got[a, l, h].bitcast(FP4X4),
                            rhs_scale=planes[h][:, (2 * a + l) * HALF : (2 * a + l + 1) * HALF],
                            start=(a == 0 and l == 0),
                            stop=(a == 1 and l == 1),
                        )
            return diffs

        def absolute(diff):
            dist = work.tile([P, HALF], F32, name="dist", bufs=6)
            nc.scalar.activation(dist[:], diff[:], ACT.Abs)
            return dist

        def fade_out(like, dist, b, t, cols):
            col = slice(PACK * b + t, PACK * b + t + 1)
            nc.scalar.activation(like[:, t, :], dist[:, cols], ACT.Exp, bias=ln_gain[:, col], scale=neg_fade[:, col])

        def quantise_h(like, key, width):
            woven = work.tile([P, width * PACK], BF16, name="woven", align_bytes=64)
            nc.vector.tensor_copy(
                woven[:].rearrange("p (c i t) -> p c t i", i=4, t=PACK),
                like[:].rearrange("p t (c i) -> p c t i", i=4),
            )
            h_codes[key] = keep.tile([P, width], U32, name="h_codes%d%d%d" % key, align_bytes=64)
            h_sc[key] = keep.tile([P, width], U8, name="h_sc%d%d%d" % key, align_bytes=64)
            nc.vector.quantize_mx(out=h_codes[key][:].bitcast(FP8X4), scales=h_sc[key][:], in_=woven[:])

        def factor_pass(acc, n, key, cols, start, stop):
            b = key[0]
            nc.tensor.matmul_mx(
                out=acc,
                lhsT=w2_w[:, b, 2 * P * n : 2 * P * (n + 1)].bitcast(FP4X4),
                lhsT_scale=w2_sc[:, b, P * n : P * (n + 1)],
                rhs=h_codes[key][:, cols].bitcast(FP8X4),
                rhs_scale=h_sc[key][:, cols],
                start=start,
                stop=stop,
            )

        QUARTER = HALF // 2
        waiting = []

        def finish_waiting():
            like, dist, key, t, width = waiting.pop()
            fade_out(like, dist, key[0], t, slice(0, width))
            if t == PACK - 1:
                quantise_h(like, key, width)

        for b in range(2):
            for h in range(2):
                width = QUARTER if b == 1 and h == 1 else HALF
                diffs = distances(b, h)
                like = keep.tile([P, PACK, width], BF16, name=f"like{b}{h}", align_bytes=64)
                dists = []
                for t in range(PACK):
                    dists.append(absolute(diffs[t]))
                    if waiting:
                        finish_waiting()
                    waiting.append((like, dists[t], (b, h, 0), t, width))
        finish_waiting()
        like = keep.tile([P, PACK, QUARTER], BF16, name="like_last", align_bytes=64)
        for t in range(PACK):
            fade_out(like, dists[t], 1, t, slice(QUARTER, HALF))
        quantise_h(like, (1, 1, 1), QUARTER)

        for n in range(2):
            acc = psum.tile([P, HALF], F32, name="acc", tag="acc", bufs=2)
            for b in range(2):
                factor_pass(acc[:], n, (b, 0, 0), slice(0, HALF), b == 0, b == 1)
            res = keep.tile([P, HALF], F32, name=f"res{n}")
            nc.vector.tensor_copy(res[:], acc[:])
            nc.sync.dma_start(out=out[P * n : P * (n + 1), 0:HALF], in_=res[:])

        for u in range(2):
            for n in range(2):
                if u == 0:
                    acc = psum.tile([P, HALF], F32, name="acc", tag="bank", bufs=6)
                else:
                    acc = psum.tile([P, HALF], F32, name="acc", tag="acc", bufs=2)
                for c in range(2):
                    first = u * QUARTER + c * P
                    factor_pass(acc[:, c * P : (c + 1) * P], n, (0, 1, 0), slice(first, first + P), c == 0, False)
                for c in range(2):
                    factor_pass(acc[:, c * P : (c + 1) * P], n, (1, 1, u), slice(c * P, (c + 1) * P), False, c == 1)
                res = keep.tile([P, QUARTER], F32, name=f"res_end{u}{n}")
                if n == 0 or u == 0:
                    nc.vector.tensor_copy(res[:], acc[:, 0:QUARTER])
                else:
                    nc.scalar.copy(res[:], acc[:, 0:QUARTER])
                first = HALF + u * QUARTER
                nc.sync.dma_start(out=out[P * n : P * (n + 1), first : first + QUARTER], in_=res[:])
